import numpy as np
CORES = [0,1,2,3,4,5,6,7]
N = 8
ROOT = 6
def setup_inputs(rng):
    return {"x": rng.standard_normal((N, 128, 128), dtype=np.float32)}
def reference(x):
    y = np.full((N, 128, N * 128), np.nan, x.dtype)
    y[ROOT] = np.concatenate(list(x), axis=1)
    return {"y": y}

N = 8
W = 128

SCRATCH = {
    "land": ("sbuf", [128, N * W], "float32"),
}
SEMAPHORES = ["loaded", "read", "arrived", "stored"]


def rank_program(g, core, T, topo):
    rank = T.rank_of(core)
    if rank is None:
        return
    root_rank = 6 if T.root is None else T.root
    root_core = T.cores[root_rank]
    mine = T.land[:, rank * W:(rank + 1) * W]

    g.sync.dma_start(mine, T.x[:]).then_inc(T.sem.loaded, 16)

    if core != root_core:
        g.wait_ge(T.sem.loaded, 16)
        rid, pid, _se = topo.addr(root_core)
        g.remote_dma(
            mine,
            mine,
            T.sem.arrived,
            T.sem.read,
            pid,
            rid,
            topo.mask(core, root_core),
        )
        g.wait_ge(T.sem.read, 16)
        return

    g.sync.wait_ge(T.sem.loaded, 16)
    g.sync.wait_ge(T.sem.arrived, 16 * (N - 1))
    g.sync.dma_start(T.y[:], T.land[:]).then_inc(T.sem.stored, 16)
    g.sync.wait_ge(T.sem.stored, 16)
